import numpy as np
CORES = [52,180,308,436]
N = 4
PERM = [[0,1],[1,2],[2,3],[3,0]]
def setup_inputs(rng):
    return {"x": rng.standard_normal((N, 128, 1024), dtype=np.float32)}
def reference(x):
    y = np.empty_like(x)
    for s, d in PERM:
        y[d] = x[s]
    return {"y": y}

@@ -1,0 +1,88 @@
+import concourse.bass as bass
+HE = 8
+PLAN = {'S': [(128, [(0, 15), (1, 240), (2, 3840), (3, 61440)]), (128, [(0, 15), (1, 240), (2, 3840), (3, 61440)])], 'C': [(32, [(4 + i, 1 << i) for i in range(8)]), (96, [(0, 15), (1, 240), (2, 3840), (3, 61440)]), (96, [(0, 15), (1, 240), (2, 3840), (3, 61440)])]}
+STORE = {'S': [0, 1], 'C': [1, 2, 0]}
+NR = max((len(v) for v in PLAN.values()))
+SCRATCH = {}
+for k_, v_ in PLAN.items():
+    for r_, (n_, us_) in enumerate(v_):
+        SCRATCH['b%s%d' % (k_, r_)] = ('dram', [len(us_), 128, n_], 'float32')
+SEMAPHORES = ['stored', 'sent'] + ['l%d' % r for r in range(NR)] + ['h%d' % r for r in range(NR)] + ['a%d' % r for r in range(NR)]
+
+def bits(m):
+    return bin(m).count('1')
+
+def routes(src, dst, topo):
+    base, me = (src - src % 8, src % 8)
+    rts = [[src, dst]] + [[src, base + 2 * q, dst] for q in range(4) if q != me // 2]
+    if topo.rack(topo.host(src)) == topo.rack(topo.host(dst)):
+        return ('S', rts)
+    for c in ((topo.chip(src) + 2) % 16, (topo.chip(src) - 2) % 16):
+        for q in range(4):
+            rts.append([src, topo.host(src) * 128 + c * 8 + 2 * q, topo.host(dst) * 128 + c * 8 + 2 * q, dst])
+    return ('C', rts)
+
+def names(T):
+    S = T.sem
+    return {'l': [lambda: S.l0, lambda: S.l1, lambda: S.l2, lambda: S.l3, lambda: S.l4, lambda: S.l5], 'h': [lambda: S.h0, lambda: S.h1, lambda: S.h2, lambda: S.h3, lambda: S.h4, lambda: S.h5], 'a': [lambda: S.a0, lambda: S.a1, lambda: S.a2, lambda: S.a3, lambda: S.a4, lambda: S.a5], 'S': [lambda: T.bS0, lambda: T.bS1, lambda: T.bS2, lambda: T.bS3, lambda: T.bS4, lambda: T.bS5], 'C': [lambda: T.bC0, lambda: T.bC1, lambda: T.bC2, lambda: T.bC3, lambda: T.bC4, lambda: T.bC5]}
+
+def relay_masks(k):
+    e = HE // k
+    return [(1 << e) - 1 << e * i for i in range(k)]
+
+def rows_of(kind):
+    out = [0]
+    for n, us in PLAN[kind]:
+        out.append(out[-1] + n * len(us) // 8)
+    return out
+
+def rank_program(g, core, T, topo):
+    perm = T.tables['PERM']
+    cores = T.cores
+    rank = T.rank_of(core)
+    N = names(T)
+
+    def send(kind, r, items, to, last):
+        rid, pid = topo.addr(to, core)
+        return [bass.RemoteDMATransfer(dst_ids=[bass.DstId(rid=rid, pnc=pid)], dma_engine_mask=m, remote_sem=N['a' if last else 'h'][r](), src=N[kind][r]()[i], dst=N[kind][r]()[i]) for i, m in items]
+    if rank is None:
+        for s, d in perm:
+            kind, rts = routes(cores[s], cores[d], topo)
+            for w, rt in enumerate(rts):
+                if core not in rt[1:-1]:
+                    continue
+                j = rt.index(core)
+                total = 0
+                for r, (n, us) in enumerate(PLAN[kind]):
+                    mine = [(i, m) for i, (ww, m) in enumerate(us) if ww == w]
+                    if not mine:
+                        continue
+                    g.wait_ge(N['h'][r](), sum((bits(m) for i, m in mine)) if j == 1 else HE)
+                    hm = relay_masks(len(mine))
+                    g.remote_dma_fused(send(kind, r, [(i, hm[q]) for q, (i, m) in enumerate(mine)], rt[j + 1], j + 2 == len(rt)), local_sem=T.sem.sent)
+                    total += HE
+                g.wait_ge(T.sem.sent, total)
+        return
+    ks, rts = [routes(cores[s], cores[d], topo) for s, d in perm if s == rank][0]
+    kr = [routes(cores[s], cores[d], topo) for s, d in perm if d == rank][0][0]
+    if ks == kr:
+        raise ValueError('a rank must send and receive over different kinds of link')
+    rows = rows_of(ks)
+    for r in range(len(PLAN[ks])):
+        g.dma_start(N[ks][r]()[:], T.x[rows[r]:rows[r + 1], :]).then_inc(N['l'][r](), 16)
+    total = 0
+    for r, (n, us) in enumerate(PLAN[ks]):
+        g.wait_ge(N['l'][r](), 16)
+        trs = []
+        for i, (w, m) in enumerate(us):
+            trs += send(ks, r, [(i, m)], rts[w][1], w == 0)
+            total += bits(m)
+        g.remote_dma_fused(trs, local_sem=T.sem.sent)
+    rows = rows_of(kr)
+    for r in STORE[kr]:
+        n, us = PLAN[kr][r]
+        cnt = sum((bits(m) for w, m in us if w == 0)) + HE * len(set((w for w, m in us if w != 0)))
+        g.wait_ge(N['a'][r](), cnt)
+        g.dma_start(T.y[rows[r]:rows[r + 1], :], N[kr][r]()[:]).then_inc(T.sem.stored, 16)
+    g.wait_ge(T.sem.stored, 16 * len(PLAN[kr]))
+    g.wait_ge(T.sem.sent, total)

@@ -2,15 +2,17 @@ import concourse.bass as bass
 HE = 8
 PLAN = {'S': [(128, [(0, 15), (1, 240), (2, 3840), (3, 61440)]), (128, [(0, 15), (1, 240), (2, 3840), (3, 61440)])], 'C': [(32, [(4 + i, 1 << i) for i in range(8)]), (96, [(0, 15), (1, 240), (2, 3840), (3, 61440)]), (96, [(0, 15), (1, 240), (2, 3840), (3, 61440)])]}
 STORE = {'S': [0, 1], 'C': [1, 2, 0]}
-NR = max((len(v) for v in PLAN.values()))
+NR = 6
 SCRATCH = {}
 for k_, v_ in PLAN.items():
     for r_, (n_, us_) in enumerate(v_):
         SCRATCH['b%s%d' % (k_, r_)] = ('dram', [len(us_), 128, n_], 'float32')
-SEMAPHORES = ['stored', 'sent'] + ['l%d' % r for r in range(NR)] + ['h%d' % r for r in range(NR)] + ['a%d' % r for r in range(NR)]
+SEMAPHORES = ['sent'] + ['%s%d' % (c, r) for c in 'lhas' for r in range(NR)]
+
 
 def bits(m):
     return bin(m).count('1')
+
 
 def routes(src, dst, topo):
     base, me = (src - src % 8, src % 8)
@@ -22,13 +24,11 @@ def routes(src, dst, topo):
             rts.append([src, topo.host(src) * 128 + c * 8 + 2 * q, topo.host(dst) * 128 + c * 8 + 2 * q, dst])
     return ('C', rts)
 
-def names(T):
-    S = T.sem
-    return {'l': [lambda: S.l0, lambda: S.l1, lambda: S.l2, lambda: S.l3, lambda: S.l4, lambda: S.l5], 'h': [lambda: S.h0, lambda: S.h1, lambda: S.h2, lambda: S.h3, lambda: S.h4, lambda: S.h5], 'a': [lambda: S.a0, lambda: S.a1, lambda: S.a2, lambda: S.a3, lambda: S.a4, lambda: S.a5], 'S': [lambda: T.bS0, lambda: T.bS1, lambda: T.bS2, lambda: T.bS3, lambda: T.bS4, lambda: T.bS5], 'C': [lambda: T.bC0, lambda: T.bC1, lambda: T.bC2, lambda: T.bC3, lambda: T.bC4, lambda: T.bC5]}
 
 def relay_masks(k):
     e = HE // k
     return [(1 << e) - 1 << e * i for i in range(k)]
+
 
 def rows_of(kind):
     out = [0]
@@ -36,15 +36,26 @@ def rows_of(kind):
         out.append(out[-1] + n * len(us) // 8)
     return out
 
+
 def rank_program(g, core, T, topo):
     perm = T.tables['PERM']
     cores = T.cores
     rank = T.rank_of(core)
-    N = names(T)
+    S = T.sem
+    sems = {'l': [S.l0, S.l1, S.l2, S.l3, S.l4, S.l5], 'h': [S.h0, S.h1, S.h2, S.h3, S.h4, S.h5],
+            'a': [S.a0, S.a1, S.a2, S.a3, S.a4, S.a5], 's': [S.s0, S.s1, S.s2, S.s3, S.s4, S.s5]}
+    bufs = {'S': [lambda: T.bS0, lambda: T.bS1, lambda: T.bS2, lambda: T.bS3, lambda: T.bS4, lambda: T.bS5],
+            'C': [lambda: T.bC0, lambda: T.bC1, lambda: T.bC2, lambda: T.bC3, lambda: T.bC4, lambda: T.bC5]}
+
+    def sem(c, r):
+        return sems[c][r]
+
+    def buf(kind, r):
+        return bufs[kind][r]()
 
     def send(kind, r, items, to, last):
         rid, pid = topo.addr(to, core)
-        return [bass.RemoteDMATransfer(dst_ids=[bass.DstId(rid=rid, pnc=pid)], dma_engine_mask=m, remote_sem=N['a' if last else 'h'][r](), src=N[kind][r]()[i], dst=N[kind][r]()[i]) for i, m in items]
+        return [bass.RemoteDMATransfer(dst_ids=[bass.DstId(rid=rid, pnc=pid)], dma_engine_mask=m, remote_sem=sem('a' if last else 'h', r), src=buf(kind, r)[i], dst=buf(kind, r)[i]) for i, m in items]
     if rank is None:
         for s, d in perm:
             kind, rts = routes(cores[s], cores[d], topo)
@@ -57,7 +68,7 @@ def rank_program(g, core, T, topo):
                     mine = [(i, m) for i, (ww, m) in enumerate(us) if ww == w]
                     if not mine:
                         continue
-                    g.wait_ge(N['h'][r](), sum((bits(m) for i, m in mine)) if j == 1 else HE)
+                    g.wait_ge(sem('h', r), sum((bits(m) for i, m in mine)) if j == 1 else HE)
                     hm = relay_masks(len(mine))
                     g.remote_dma_fused(send(kind, r, [(i, hm[q]) for q, (i, m) in enumerate(mine)], rt[j + 1], j + 2 == len(rt)), local_sem=T.sem.sent)
                     total += HE
@@ -67,22 +78,25 @@ def rank_program(g, core, T, topo):
     kr = [routes(cores[s], cores[d], topo) for s, d in perm if d == rank][0][0]
     if ks == kr:
         raise ValueError('a rank must send and receive over different kinds of link')
+    qs = [g.sync, g.scalar]
     rows = rows_of(ks)
     for r in range(len(PLAN[ks])):
-        g.dma_start(N[ks][r]()[:], T.x[rows[r]:rows[r + 1], :]).then_inc(N['l'][r](), 16)
+        qs[r % 2].dma_start(buf(ks, r)[:], T.x[rows[r]:rows[r + 1], :]).then_inc(sem('l', r), 16)
+    rows = rows_of(kr)
+    for k, r in enumerate(STORE[kr]):
+        n, us = PLAN[kr][r]
+        cnt = sum((bits(m) for w, m in us if w == 0)) + HE * len(set((w for w, m in us if w != 0)))
+        q = qs[(k + len(PLAN[ks])) % 2]
+        q.wait_ge(sem('a', r), cnt)
+        q.dma_start(T.y[rows[r]:rows[r + 1], :], buf(kr, r)[:]).then_inc(sem('s', r), 16)
     total = 0
     for r, (n, us) in enumerate(PLAN[ks]):
-        g.wait_ge(N['l'][r](), 16)
+        g.wait_ge(sem('l', r), 16)
         trs = []
         for i, (w, m) in enumerate(us):
             trs += send(ks, r, [(i, m)], rts[w][1], w == 0)
             total += bits(m)
         g.remote_dma_fused(trs, local_sem=T.sem.sent)
-    rows = rows_of(kr)
-    for r in STORE[kr]:
-        n, us = PLAN[kr][r]
-        cnt = sum((bits(m) for w, m in us if w == 0)) + HE * len(set((w for w, m in us if w != 0)))
-        g.wait_ge(N['a'][r](), cnt)
-        g.dma_start(T.y[rows[r]:rows[r + 1], :], N[kr][r]()[:]).then_inc(T.sem.stored, 16)
-    g.wait_ge(T.sem.stored, 16 * len(PLAN[kr]))
     g.wait_ge(T.sem.sent, total)
+    for r in STORE[kr]:
+        g.wait_ge(sem('s', r), 16)

@@ -1,12 +1,14 @@
 import concourse.bass as bass
 HE = 8
-PLAN = {'S': [(128, [(0, 15), (1, 240), (2, 3840), (3, 61440)]), (128, [(0, 15), (1, 240), (2, 3840), (3, 61440)])], 'C': [(32, [(4 + i, 1 << i) for i in range(8)]), (96, [(0, 15), (1, 240), (2, 3840), (3, 61440)]), (96, [(0, 15), (1, 240), (2, 3840), (3, 61440)])]}
-STORE = {'S': [0, 1], 'C': [1, 2, 0]}
+MEM = 'dram'
+Q4 = [(0, 15), (1, 240), (2, 3840), (3, 61440)]
+PLAN = {'S': [(64, Q4)] * 4, 'C': [(32, [(4 + i, 1 << i) for i in range(8)])] + [(64, Q4)] * 3}
+STORE = {'S': [0, 1, 2, 3], 'C': [1, 2, 3, 0]}
 NR = 6
 SCRATCH = {}
 for k_, v_ in PLAN.items():
     for r_, (n_, us_) in enumerate(v_):
-        SCRATCH['b%s%d' % (k_, r_)] = ('dram', [len(us_), 128, n_], 'float32')
+        SCRATCH['b%s%d' % (k_, r_)] = ('dram', [len(us_), 128, n_], 'float32') if MEM == 'dram' else ('sbuf', [128, len(us_) * n_], 'float32')
 SEMAPHORES = ['sent'] + ['%s%d' % (c, r) for c in 'lhas' for r in range(NR)]
 
 
@@ -33,7 +35,7 @@ def relay_masks(k):
 def rows_of(kind):
     out = [0]
     for n, us in PLAN[kind]:
-        out.append(out[-1] + n * len(us) // 8)
+        out.append(out[-1] + n * len(us) // (8 if MEM == 'dram' else 1))
     return out
 
 
@@ -53,9 +55,18 @@ def rank_program(g, core, T, topo):
     def buf(kind, r):
         return bufs[kind][r]()
 
+    def piece(kind, r, i):
+        if MEM == 'dram':
+            return buf(kind, r)[i]
+        n = PLAN[kind][r][0]
+        return buf(kind, r)[:, i * n:(i + 1) * n]
+
+    def part(t, a, b):
+        return t[a:b, :] if MEM == 'dram' else t[:, a:b]
+
     def send(kind, r, items, to, last):
         rid, pid = topo.addr(to, core)
-        return [bass.RemoteDMATransfer(dst_ids=[bass.DstId(rid=rid, pnc=pid)], dma_engine_mask=m, remote_sem=sem('a' if last else 'h', r), src=buf(kind, r)[i], dst=buf(kind, r)[i]) for i, m in items]
+        return [bass.RemoteDMATransfer(dst_ids=[bass.DstId(rid=rid, pnc=pid)], dma_engine_mask=m, remote_sem=sem('a' if last else 'h', r), src=piece(kind, r, i), dst=piece(kind, r, i)) for i, m in items]
     if rank is None:
         for s, d in perm:
             kind, rts = routes(cores[s], cores[d], topo)
@@ -81,14 +92,14 @@ def rank_program(g, core, T, topo):
     qs = [g.sync, g.scalar]
     rows = rows_of(ks)
     for r in range(len(PLAN[ks])):
-        qs[r % 2].dma_start(buf(ks, r)[:], T.x[rows[r]:rows[r + 1], :]).then_inc(sem('l', r), 16)
+        qs[r % 2].dma_start(buf(ks, r)[:], part(T.x, rows[r], rows[r + 1])).then_inc(sem('l', r), 16)
     rows = rows_of(kr)
     for k, r in enumerate(STORE[kr]):
         n, us = PLAN[kr][r]
         cnt = sum((bits(m) for w, m in us if w == 0)) + HE * len(set((w for w, m in us if w != 0)))
         q = qs[(k + len(PLAN[ks])) % 2]
         q.wait_ge(sem('a', r), cnt)
-        q.dma_start(T.y[rows[r]:rows[r + 1], :], buf(kr, r)[:]).then_inc(sem('s', r), 16)
+        q.dma_start(part(T.y, rows[r], rows[r + 1]), buf(kr, r)[:]).then_inc(sem('s', r), 16)
     total = 0
     for r, (n, us) in enumerate(PLAN[ks]):
         g.wait_ge(sem('l', r), 16)

@@ -2,8 +2,11 @@ import concourse.bass as bass
 HE = 8
 MEM = 'dram'
 Q4 = [(0, 15), (1, 240), (2, 3840), (3, 61440)]
-PLAN = {'S': [(64, Q4)] * 4, 'C': [(32, [(4 + i, 1 << i) for i in range(8)])] + [(64, Q4)] * 3}
-STORE = {'S': [0, 1, 2, 3], 'C': [1, 2, 3, 0]}
+M4 = [(0, 0x000F), (1, 0x0F00), (2, 0x3000), (3, 0xC000)]
+G1 = [(4 + i, 3 << 2 * i) for i in range(4)]
+G2 = [(8 + i, 3 << 2 * i) for i in range(4)]
+PLAN = {'S': [(64, Q4)] * 4, 'C': [(48, G1), (32, G2)] + [(54, M4)] * 3 + [(56, [(0, 255)])]}
+STORE = {'S': [(0, 0), (1, 1), (2, 0), (3, 1)], 'C': [(0, 1), (1, 1), (2, 0), (3, 0), (4, 0), (5, 0)]}
 NR = 6
 SCRATCH = {}
 for k_, v_ in PLAN.items():
@@ -83,7 +86,8 @@ def rank_program(g, core, T, topo):
                     hm = relay_masks(len(mine))
                     g.remote_dma_fused(send(kind, r, [(i, hm[q]) for q, (i, m) in enumerate(mine)], rt[j + 1], j + 2 == len(rt)), local_sem=T.sem.sent)
                     total += HE
-                g.wait_ge(T.sem.sent, total)
+                if total:
+                    g.wait_ge(T.sem.sent, total)
         return
     ks, rts = [routes(cores[s], cores[d], topo) for s, d in perm if s == rank][0]
     kr = [routes(cores[s], cores[d], topo) for s, d in perm if d == rank][0][0]
@@ -94,12 +98,11 @@ def rank_program(g, core, T, topo):
     for r in range(len(PLAN[ks])):
         qs[r % 2].dma_start(buf(ks, r)[:], part(T.x, rows[r], rows[r + 1])).then_inc(sem('l', r), 16)
     rows = rows_of(kr)
-    for k, r in enumerate(STORE[kr]):
+    for r, q in STORE[kr]:
         n, us = PLAN[kr][r]
         cnt = sum((bits(m) for w, m in us if w == 0)) + HE * len(set((w for w, m in us if w != 0)))
-        q = qs[(k + len(PLAN[ks])) % 2]
-        q.wait_ge(sem('a', r), cnt)
-        q.dma_start(part(T.y, rows[r], rows[r + 1]), buf(kr, r)[:]).then_inc(sem('s', r), 16)
+        qs[q].wait_ge(sem('a', r), cnt)
+        qs[q].dma_start(part(T.y, rows[r], rows[r + 1]), buf(kr, r)[:]).then_inc(sem('s', r), 16)
     total = 0
     for r, (n, us) in enumerate(PLAN[ks]):
         g.wait_ge(sem('l', r), 16)
@@ -109,5 +112,5 @@ def rank_program(g, core, T, topo):
             total += bits(m)
         g.remote_dma_fused(trs, local_sem=T.sem.sent)
     g.wait_ge(T.sem.sent, total)
-    for r in STORE[kr]:
+    for r, q in STORE[kr]:
         g.wait_ge(sem('s', r), 16)

@@ -2,11 +2,15 @@ import concourse.bass as bass
 HE = 8
 MEM = 'dram'
 Q4 = [(0, 15), (1, 240), (2, 3840), (3, 61440)]
-M4 = [(0, 0x000F), (1, 0x0F00), (2, 0x3000), (3, 0xC000)]
+LANES = [1, 2, 3, 16]
+O4 = [(w, 3 << 8 + 2 * i) for i, w in enumerate(LANES)]
+O8 = [(w, 1 << 8 + 2 * i + j) for i, w in enumerate(LANES) for j in range(2)]
 G1 = [(4 + i, 3 << 2 * i) for i in range(4)]
 G2 = [(8 + i, 3 << 2 * i) for i in range(4)]
-PLAN = {'S': [(64, Q4)] * 4, 'C': [(48, G1), (32, G2)] + [(54, M4)] * 3 + [(56, [(0, 255)])]}
-STORE = {'S': [(0, 0), (1, 1), (2, 0), (3, 1)], 'C': [(0, 1), (1, 1), (2, 0), (3, 0), (4, 0), (5, 0)]}
+G3 = [(12 + i, 3 << 2 * i) for i in range(4)]
+PLAN = {'S': [(64, Q4)] * 4, 'C': [(48, G1), (48, O8), (36, G2), (36, O4), (20, G3), (20, O4)]}
+FUSE = {'S': [[0], [1], [2], [3]], 'C': [[0, 1], [2, 3], [4, 5]]}
+STORE = {'S': [(0, 0), (1, 1), (2, 0), (3, 1)], 'C': [(0, 1), (2, 1), (4, 1), (1, 0), (3, 0), (5, 0)]}
 NR = 6
 SCRATCH = {}
 for k_, v_ in PLAN.items():
@@ -24,9 +28,10 @@ def routes(src, dst, topo):
     rts = [[src, dst]] + [[src, base + 2 * q, dst] for q in range(4) if q != me // 2]
     if topo.rack(topo.host(src)) == topo.rack(topo.host(dst)):
         return ('S', rts)
-    for c in ((topo.chip(src) + 2) % 16, (topo.chip(src) - 2) % 16):
+    for c in ((topo.chip(src) + 2) % 16, (topo.chip(src) - 2) % 16, (topo.chip(src) + 4) % 16):
         for q in range(4):
             rts.append([src, topo.host(src) * 128 + c * 8 + 2 * q, topo.host(dst) * 128 + c * 8 + 2 * q, dst])
+    rts.append([src, src ^ 1, dst])
     return ('C', rts)
 
 
@@ -104,12 +109,13 @@ def rank_program(g, core, T, topo):
         qs[q].wait_ge(sem('a', r), cnt)
         qs[q].dma_start(part(T.y, rows[r], rows[r + 1]), buf(kr, r)[:]).then_inc(sem('s', r), 16)
     total = 0
-    for r, (n, us) in enumerate(PLAN[ks]):
-        g.wait_ge(sem('l', r), 16)
+    for group in FUSE[ks]:
         trs = []
-        for i, (w, m) in enumerate(us):
-            trs += send(ks, r, [(i, m)], rts[w][1], w == 0)
-            total += bits(m)
+        for r in group:
+            g.wait_ge(sem('l', r), 16)
+            for i, (w, m) in enumerate(PLAN[ks][r][1]):
+                trs += send(ks, r, [(i, m)], rts[w][1], w == 0)
+                total += bits(m)
         g.remote_dma_fused(trs, local_sem=T.sem.sent)
     g.wait_ge(T.sem.sent, total)
     for r, q in STORE[kr]:

@@ -1,21 +1,21 @@
 import concourse.bass as bass
+
 HE = 8
-MEM = 'dram'
-Q4 = [(0, 15), (1, 240), (2, 3840), (3, 61440)]
-LANES = [1, 2, 3, 16]
-O4 = [(w, 3 << 8 + 2 * i) for i, w in enumerate(LANES)]
-O8 = [(w, 1 << 8 + 2 * i + j) for i, w in enumerate(LANES) for j in range(2)]
+Q4 = [(0, 0x000F), (1, 0x00F0), (2, 0x0F00), (3, 0xF000)]
+NEAR = [1, 2, 3, 16]
+O4 = [(w, 3 << 8 + 2 * i) for i, w in enumerate(NEAR)]
+O8 = [(w, 1 << 8 + 2 * i + j) for i, w in enumerate(NEAR) for j in range(2)]
 G1 = [(4 + i, 3 << 2 * i) for i in range(4)]
 G2 = [(8 + i, 3 << 2 * i) for i in range(4)]
 G3 = [(12 + i, 3 << 2 * i) for i in range(4)]
-PLAN = {'S': [(64, Q4)] * 4, 'C': [(48, G1), (48, O8), (36, G2), (36, O4), (20, G3), (20, O4)]}
+PLAN = {'S': [(64, Q4)] * 4, 'C': [(44, G1), (44, O4), (40, G2), (40, O8), (24, G3), (24, O4)]}
 FUSE = {'S': [[0], [1], [2], [3]], 'C': [[0, 1], [2, 3], [4, 5]]}
 STORE = {'S': [(0, 0), (1, 1), (2, 0), (3, 1)], 'C': [(0, 1), (2, 1), (4, 1), (1, 0), (3, 0), (5, 0)]}
 NR = 6
 SCRATCH = {}
 for k_, v_ in PLAN.items():
     for r_, (n_, us_) in enumerate(v_):
-        SCRATCH['b%s%d' % (k_, r_)] = ('dram', [len(us_), 128, n_], 'float32') if MEM == 'dram' else ('sbuf', [128, len(us_) * n_], 'float32')
+        SCRATCH['b%s%d' % (k_, r_)] = ('dram', [len(us_), 128, n_], 'float32')
 SEMAPHORES = ['sent'] + ['%s%d' % (c, r) for c in 'lhas' for r in range(NR)]
 
 
@@ -43,7 +43,7 @@ def relay_masks(k):
 def rows_of(kind):
     out = [0]
     for n, us in PLAN[kind]:
-        out.append(out[-1] + n * len(us) // (8 if MEM == 'dram' else 1))
+        out.append(out[-1] + n * len(us) // 8)
     return out
 
 
@@ -63,18 +63,9 @@ def rank_program(g, core, T, topo):
     def buf(kind, r):
         return bufs[kind][r]()
 
-    def piece(kind, r, i):
-        if MEM == 'dram':
-            return buf(kind, r)[i]
-        n = PLAN[kind][r][0]
-        return buf(kind, r)[:, i * n:(i + 1) * n]
-
-    def part(t, a, b):
-        return t[a:b, :] if MEM == 'dram' else t[:, a:b]
-
     def send(kind, r, items, to, last):
         rid, pid = topo.addr(to, core)
-        return [bass.RemoteDMATransfer(dst_ids=[bass.DstId(rid=rid, pnc=pid)], dma_engine_mask=m, remote_sem=sem('a' if last else 'h', r), src=piece(kind, r, i), dst=piece(kind, r, i)) for i, m in items]
+        return [bass.RemoteDMATransfer(dst_ids=[bass.DstId(rid=rid, pnc=pid)], dma_engine_mask=m, remote_sem=sem('a' if last else 'h', r), src=buf(kind, r)[i], dst=buf(kind, r)[i]) for i, m in items]
     if rank is None:
         for s, d in perm:
             kind, rts = routes(cores[s], cores[d], topo)
@@ -101,13 +92,13 @@ def rank_program(g, core, T, topo):
     qs = [g.sync, g.scalar]
     rows = rows_of(ks)
     for r in range(len(PLAN[ks])):
-        qs[r % 2].dma_start(buf(ks, r)[:], part(T.x, rows[r], rows[r + 1])).then_inc(sem('l', r), 16)
+        qs[r % 2].dma_start(buf(ks, r)[:], T.x[rows[r]:rows[r + 1], :]).then_inc(sem('l', r), 16)
     rows = rows_of(kr)
     for r, q in STORE[kr]:
         n, us = PLAN[kr][r]
         cnt = sum((bits(m) for w, m in us if w == 0)) + HE * len(set((w for w, m in us if w != 0)))
         qs[q].wait_ge(sem('a', r), cnt)
-        qs[q].dma_start(part(T.y, rows[r], rows[r + 1]), buf(kr, r)[:]).then_inc(sem('s', r), 16)
+        qs[q].dma_start(T.y[rows[r]:rows[r + 1], :], buf(kr, r)[:]).then_inc(sem('s', r), 16)
     total = 0
     for group in FUSE[ks]:
         trs = []

import concourse.bass as bass

HE = 8
Q4 = [(0, 0x000F), (1, 0x00F0), (2, 0x0F00), (3, 0xF000)]
NEAR = [1, 2, 3, 16]
O4 = [(w, 3 << 8 + 2 * i) for i, w in enumerate(NEAR)]
O8 = [(w, 1 << 8 + 2 * i + j) for i, w in enumerate(NEAR) for j in range(2)]
G1 = [(4 + i, 3 << 2 * i) for i in range(4)]
G2 = [(8 + i, 3 << 2 * i) for i in range(4)]
G3 = [(12 + i, 3 << 2 * i) for i in range(4)]
PLAN = {'S': [(64, Q4)] * 4, 'C': [(44, G1), (44, O4), (40, G2), (40, O8), (24, G3), (24, O4)]}
FUSE = {'S': [[0], [1], [2], [3]], 'C': [[0, 1], [2, 3], [4, 5]]}
STORE = {'S': [(0, 0), (1, 1), (2, 0), (3, 1)], 'C': [(0, 1), (2, 1), (4, 1), (1, 0), (3, 0), (5, 0)]}
NR = 6
SCRATCH = {}
for k_, v_ in PLAN.items():
    for r_, (n_, us_) in enumerate(v_):
        SCRATCH['b%s%d' % (k_, r_)] = ('dram', [len(us_), 128, n_], 'float32')
SEMAPHORES = ['sent'] + ['%s%d' % (c, r) for c in 'lhas' for r in range(NR)]


def bits(m):
    return bin(m).count('1')


def routes(src, dst, topo):
    base, me = (src - src % 8, src % 8)
    rts = [[src, dst]] + [[src, base + 2 * q, dst] for q in range(4) if q != me // 2]
    if topo.rack(topo.host(src)) == topo.rack(topo.host(dst)):
        return ('S', rts)
    for c in ((topo.chip(src) + 2) % 16, (topo.chip(src) - 2) % 16, (topo.chip(src) + 4) % 16):
        for q in range(4):
            rts.append([src, topo.host(src) * 128 + c * 8 + 2 * q, topo.host(dst) * 128 + c * 8 + 2 * q, dst])
    rts.append([src, src ^ 1, dst])
    return ('C', rts)


def relay_masks(k):
    e = HE // k
    return [(1 << e) - 1 << e * i for i in range(k)]


def rows_of(kind):
    out = [0]
    for n, us in PLAN[kind]:
        out.append(out[-1] + n * len(us) // 8)
    return out


def rank_program(g, core, T, topo):
    perm = T.tables['PERM']
    cores = T.cores
    rank = T.rank_of(core)
    S = T.sem
    sems = {'l': [S.l0, S.l1, S.l2, S.l3, S.l4, S.l5], 'h': [S.h0, S.h1, S.h2, S.h3, S.h4, S.h5],
            'a': [S.a0, S.a1, S.a2, S.a3, S.a4, S.a5], 's': [S.s0, S.s1, S.s2, S.s3, S.s4, S.s5]}
    bufs = {'S': [lambda: T.bS0, lambda: T.bS1, lambda: T.bS2, lambda: T.bS3, lambda: T.bS4, lambda: T.bS5],
            'C': [lambda: T.bC0, lambda: T.bC1, lambda: T.bC2, lambda: T.bC3, lambda: T.bC4, lambda: T.bC5]}

    def sem(c, r):
        return sems[c][r]

    def buf(kind, r):
        return bufs[kind][r]()

    def send(kind, r, items, to, last):
        rid, pid = topo.addr(to, core)
        return [bass.RemoteDMATransfer(dst_ids=[bass.DstId(rid=rid, pnc=pid)], dma_engine_mask=m, remote_sem=sem('a' if last else 'h', r), src=buf(kind, r)[i], dst=buf(kind, r)[i]) for i, m in items]
    if rank is None:
        for s, d in perm:
            kind, rts = routes(cores[s], cores[d], topo)
            for w, rt in enumerate(rts):
                if core not in rt[1:-1]:
                    continue
                j = rt.index(core)
                total = 0
                for r, (n, us) in enumerate(PLAN[kind]):
                    mine = [(i, m) for i, (ww, m) in enumerate(us) if ww == w]
                    if not mine:
                        continue
                    g.wait_ge(sem('h', r), sum((bits(m) for i, m in mine)) if j == 1 else HE)
                    hm = relay_masks(len(mine))
                    g.remote_dma_fused(send(kind, r, [(i, hm[q]) for q, (i, m) in enumerate(mine)], rt[j + 1], j + 2 == len(rt)), local_sem=T.sem.sent)
                    total += HE
                if total:
                    g.wait_ge(T.sem.sent, total)
        return
    ks, rts = [routes(cores[s], cores[d], topo) for s, d in perm if s == rank][0]
    kr = [routes(cores[s], cores[d], topo) for s, d in perm if d == rank][0][0]
    if ks == kr:
        raise ValueError('a rank must send and receive over different kinds of link')
    qs = [g.sync, g.scalar]
    rows = rows_of(ks)
    for r in range(len(PLAN[ks])):
        qs[r % 2].dma_start(buf(ks, r)[:], T.x[rows[r]:rows[r + 1], :]).then_inc(sem('l', r), 16)
    rows = rows_of(kr)
    for r, q in STORE[kr]:
        n, us = PLAN[kr][r]
        cnt = sum((bits(m) for w, m in us if w == 0)) + HE * len(set((w for w, m in us if w != 0)))
        qs[q].wait_ge(sem('a', r), cnt)
        qs[q].dma_start(T.y[rows[r]:rows[r + 1], :], buf(kr, r)[:]).then_inc(sem('s', r), 16)
    total = 0
    for group in FUSE[ks]:
        trs = []
        for r in group:
            g.wait_ge(sem('l', r), 16)
            for i, (w, m) in enumerate(PLAN[ks][r][1]):
                trs += send(ks, r, [(i, m)], rts[w][1], w == 0)
                total += bits(m)
        g.remote_dma_fused(trs, local_sem=T.sem.sent)
    g.wait_ge(T.sem.sent, total)
    for r, q in STORE[kr]:
        g.wait_ge(sem('s', r), 16)
